import numpy as np
import ml_dtypes


def mxq(x, axis, fmt="e4m3"):
    dtype, down = {"e4m3": (ml_dtypes.float8_e4m3fn, 7), "e5m2": (ml_dtypes.float8_e5m2, 14)}[fmt]
    v = np.moveaxis(np.asarray(x, np.float32).astype(ml_dtypes.bfloat16).astype(np.float64), axis, -1)
    blocks = v.reshape(v.shape[:-1] + (-1, 32))
    amax = np.abs(blocks).max(-1, keepdims=True)
    byte = np.maximum(np.where(amax > 0, np.frexp(amax)[1] - 1 + 127, 0) - down, 1)
    scale = np.exp2(byte - 127.0)
    codes = (blocks / scale).astype(np.float32).astype(dtype).astype(np.float64)
    return np.moveaxis((codes * scale).reshape(v.shape), -1, axis)


WIDE = False


def mx_kscale(k):
    if not WIDE:
        return np.ones(k)
    levels = np.array([10, -10, 5, -5, 0])
    if k % 512:
        return np.exp2(np.random.permutation(np.resize(levels, k // 32))).repeat(32)
    a = np.empty((k // 512, 16))
    for p in range(k // 512):
        a[p, :8] = np.random.permutation(np.resize(levels, 8))
        for g in range(8):
            far = levels[np.abs(levels - a[p, g]) >= 10]
            a[p, g + 8] = far[np.random.randint(len(far))]
    return np.exp2(a.ravel()).repeat(32)


def f64(x):
    return np.asarray(x).astype(np.float64)


def striped(idx):
    return np.tile(idx.reshape(-1, 16).T, (8, 1)).astype(np.uint16)


def unstriped(offs):
    return offs[:16].T.reshape(-1).astype(np.int64)


E2M1 = np.array([0.0, 0.5, 1.0, 1.5, 2.0, 3.0, 4.0, 6.0, -0.0, -0.5, -1.0, -1.5, -2.0, -3.0, -4.0, -6.0])


def pack_fp4(w):
    k, n = w.shape
    w = f64(np.asarray(w, np.float32).astype(ml_dtypes.bfloat16)).reshape(k // 32, 32, n)
    amax = np.abs(w).max(1)
    mant, ex = np.frexp(amax / 6.0)
    byte = np.clip(np.where(amax > 0, np.where(mant > 0.5, ex, ex - 1) + 127, 1), 1, 254)
    scaled = (w * np.exp2(127.0 - byte)[:, None, :]).reshape(k, n).astype(np.float32)
    c = np.ascontiguousarray(scaled.reshape(k // 512, 128, 4, n).transpose(0, 1, 3, 2)).astype(ml_dtypes.float4_e2m1fn).view(np.uint8) & 0xF
    words = (c[..., 0::2] | (c[..., 1::2] << 4)).reshape(k // 512, 128, 2 * n)
    return np.ascontiguousarray(words), np.ascontiguousarray(byte.astype(np.uint8).reshape(k // 512, 16, n))


def unpack_fp4(words, scales):
    g, _, n = scales.shape
    words = np.ascontiguousarray(words).reshape(g, 128, n, 2)
    nib = np.empty((g, 128, n, 4), np.uint8)
    nib[..., 0::2] = words & 0xF
    nib[..., 1::2] = words >> 4
    vals = E2M1[nib] * np.repeat(np.exp2(scales.astype(np.float64) - 127.0), 8, axis=1)[..., None]
    return vals.transpose(0, 1, 3, 2).reshape(g * 512, n)


def relu(v):
    return np.maximum(v, 0.0)


K, T, S, D, V, N = 1024, 2048, 1024, 3, 512, 256
P = 2 ** 7


def setup_inputs():
    n = np.random.standard_normal
    s = mx_kscale(K)[:, None]
    packed_w1 = pack_fp4(n((K, N)) / np.sqrt(K) / s)
    return {
        "xT": (n((K, T)) * s).astype(np.float32),
        "w1_words": packed_w1[0],
        "w1_scales": packed_w1[1],
        "score": np.tile(np.random.standard_normal((D, 1, V)), (1, P, 1)).astype(np.float32),
        "offs": striped(np.random.permutation(T)[:S]),
        "pos1": striped(np.random.permutation(S)[:V]),
        "pos2": striped(np.random.permutation(S)[:V]),
        "pos3": striped(np.random.permutation(S)[:V]),
    }


def reference(xT, w1_words, w1_scales, score, offs, pos1, pos2, pos3):
    xq = mxq(f64(xT)[:, unstriped(offs)], 0, "e4m3")
    y = unpack_fp4(w1_words, w1_scales).T @ xq
    e0 = np.exp(f64(score)[0, :1])
    e1 = np.exp(f64(score)[1, :1])
    e2 = np.exp(f64(score)[2, :1])
    num = y[:, unstriped(pos1)] * e0 + y[:, unstriped(pos2)] * e1 + y[:, unstriped(pos3)] * e2
    den = e0 + e1 + e2
    return relu(num / den)

@@ -1,0 +1,247 @@
+from contextlib import ExitStack
+
+import concourse.mybir as mybir
+from concourse.masks import make_identity
+
+K, T, S, D, V, N = 1024, 2048, 1024, 3, 512, 256
+FLOPS = 2 * K * S * N
+
+F32 = mybir.dt.float32
+BF16 = mybir.dt.bfloat16
+I32 = mybir.dt.int32
+U32 = mybir.dt.uint32
+U16 = mybir.dt.uint16
+U8 = mybir.dt.uint8
+FP8X4 = mybir.dt.float8_e4m3fn_x4
+FP4X4 = mybir.dt.float4_e2m1fn_x4
+ALU = mybir.AluOpType
+ACT = mybir.ActivationFunctionType
+AX = mybir.AxisListType
+
+P = 128
+PASSES = 2
+BLOCKS = N // P
+QUARTER = S // 4
+HALF_V = V // 2
+
+CHUNKS = (
+    ((1024, 0), (1024, 320)),
+    ((1024, 1024), (1024, 320)),
+    ((1024, 1024), (1024, 320)),
+    ((1024, 896), (512, 0), (256, 0), (256, 96)),
+)
+WINDOW_START = (3584, 2240, 896, 0)
+
+
+def tile_picked_gatv_relu_e_kernel(
+    tc, xT, w1_words, w1_scales, score, offs, pos1, pos2, pos3, out
+):
+    nc = tc.nc
+    with ExitStack() as ctx:
+        keep = ctx.enter_context(tc.tile_pool(name="keep", bufs=1))
+        psum = ctx.enter_context(tc.psum_pool(name="psum", bufs=1))
+
+        def bank(i, shape, name):
+            return psum.tile(shape, F32, tag="bank%d" % i, name=name)
+
+        offs_sb = keep.tile([P, S // 16], U16, name="offs_sb")
+        pos_sb = [keep.tile([P, V // 16], U16, name="pos_sb%d" % d) for d in range(D)]
+        w_scales = keep.tile([P, PASSES, N], U8, name="w_scales", align_bytes=64)
+        score_rows = keep.tile([P, P], F32, name="score_rows")
+        ident = keep.tile([P, P], F32, name="ident")
+
+        nc.gpsimd.memset(w_scales[:].bitcast(I32), 0)
+        make_identity(nc, ident[:])
+
+        x_rows = xT.rearrange("(z p u e) t -> z u p e t", z=PASSES, p=P, u=2, e=2)
+        raw = {}
+
+        def load_x(pair, i):
+            start = sum(c[0] for c in CHUNKS[pair][:i])
+            width = CHUNKS[pair][i][0]
+            t = keep.tile([P, 2, width], F32, name="raw%d_%d" % (pair, i), tag="raw%d_%d" % (pair, i), align_bytes=64)
+            nc.sync.dma_start(out=t[:], in_=x_rows[pair // 2, pair % 2, :, :, start : start + width])
+            raw[pair, i] = (t, start)
+
+        def load_scales(q):
+            nc.sync.dma_start(
+                out=w_scales[32 * q : 32 * q + 4, :, :].bitcast(I32),
+                in_=w1_scales[:, 4 * q : 4 * q + 4, :].rearrange("z r c -> r z c").bitcast(I32),
+            )
+
+        score_runs = score.rearrange("d r (c p) -> (d r c) p", p=P)
+        nc.sync.dma_start(out=score_rows[:], in_=score_runs[0 : 9 * (P - 1) + 1 : 9, :])
+        load_x(0, 0)
+        load_x(0, 1)
+        nc.sync.dma_start(offs_sb[:], offs)
+        load_x(1, 0)
+        load_scales(0)
+        load_scales(1)
+        load_x(1, 1)
+        load_scales(2)
+        load_scales(3)
+        load_x(2, 0)
+        load_x(2, 1)
+        for i in range(len(CHUNKS[3])):
+            load_x(3, i)
+        for d, pos in enumerate((pos1, pos2, pos3)):
+            nc.sync.dma_start(pos_sb[d][:], pos)
+
+        def cast(pair):
+            for i, (width, on_scalar) in enumerate(CHUNKS[pair]):
+                t, start = raw[pair, i]
+                src = t[:].rearrange("p e c -> p c e")
+                first = WINDOW_START[pair] + start
+                dst = windows[:, 2 * first : 2 * (first + width)].rearrange("p (c e) -> p c e", e=2)
+                if on_scalar > 0:
+                    nc.scalar.copy(out=dst[:, :on_scalar, :], in_=src[:, :on_scalar, :])
+                if on_scalar < width:
+                    nc.vector.tensor_copy(out=dst[:, on_scalar:, :], in_=src[:, on_scalar:, :])
+
+        def looked_up(pair, first, count):
+            words = windows[:, 2 * WINDOW_START[pair] : 2 * (WINDOW_START[pair] + T)].bitcast(U32)
+            return words.indirect(offs_sb[:, first // 16 : (first + count) // 16])
+
+        def word_pairs(t):
+            return t[:].bitcast(U32).rearrange("p (s u) -> p s u", u=2)
+
+        codes = [keep.tile([P, S], U32, name="codes%d" % z, tag="codes%d" % z, align_bytes=64) for z in range(PASSES)]
+        x_scales = [keep.tile([P, S], U8, name="x_scales%d" % z, align_bytes=64) for z in range(PASSES)]
+
+        def quantize(z, first, count, src):
+            cols = slice(first, first + count)
+            nc.vector.quantize_mx(out=codes[z][:, cols].bitcast(FP8X4), scales=x_scales[z][:, cols], in_=src)
+
+        groups = [(0, 0, 512), (1, 0, 512), (0, 512, 128), (0, 640, 128), (0, 768, 128), (0, 896, 128), (1, 512, 512)]
+
+        def multiply(i, z):
+            b, first, count = groups[i]
+            cols = slice(first, first + count)
+            nc.tensor.matmul_mx(
+                out=acc[i][:],
+                lhsT=w_words[:, z, 2 * P * b : 2 * P * (b + 1)].bitcast(FP4X4),
+                lhsT_scale=w_scales[:, z, P * b : P * (b + 1)],
+                rhs=codes[z][:, cols].bitcast(FP8X4),
+                rhs_scale=x_scales[z][:, cols],
+                start=(z == 0),
+                stop=(z == PASSES - 1),
+            )
+
+        score_t = bank(7, [P, D, 60], "score_t")
+        nc.tensor.transpose(score_t[:].rearrange("p d j -> p (d j)")[:, 0:P], score_rows[:], ident[:])
+        top = keep.tile([P, 4], F32, name="top")
+        shifted = keep.tile([P, D, 4], F32, name="shifted")
+        expo = keep.tile([P, D, 4], F32, name="expo")
+        total = keep.tile([P, 4], F32, name="total")
+        inverse = keep.tile([P, 4], F32, name="inverse", tag="window0", align_bytes=64)
+        weight = keep.tile([P, D, 4], F32, name="weight")
+        nc.vector.tensor_reduce(out=top[:], in_=score_t[:, :, 0:4].rearrange("p d c -> p c d"), axis=AX.X, op=ALU.max)
+        nc.vector.tensor_tensor(
+            out=shifted[:], in0=score_t[:, :, 0:4], in1=top[:].unsqueeze(1).to_broadcast([P, D, 4]), op=ALU.subtract
+        )
+        nc.scalar.activation(out=expo[:], in_=shifted[:], func=ACT.Exp)
+        nc.vector.tensor_reduce(out=total[:], in_=expo[:].rearrange("p d c -> p c d"), axis=AX.X, op=ALU.add)
+        nc.vector.reciprocal(out=inverse[:], in_=total[:])
+        nc.vector.tensor_tensor(
+            out=weight[:], in0=expo[:], in1=inverse[:].unsqueeze(1).to_broadcast([P, D, 4]), op=ALU.mult
+        )
+
+        spread = [keep.tile([P, HALF_V], F32, name="spread%d" % d) for d in range(D)]
+        for d in range(D):
+            spread_t = bank(d, [P, HALF_V], "spread_t%d" % d)
+            for c in range(2):
+                nc.tensor.transpose(spread_t[:, P * c : P * (c + 1)], weight[:, d, 2 + c : 3 + c].to_broadcast([P, P]), ident[:])
+            nc.vector.tensor_copy(out=spread[d][:], in_=spread_t[:])
+
+        acc = [bank(i, [P, g[2]], "acc%d" % i) for i, g in enumerate(groups)]
+        windows = keep.tile([P, 2 * (WINDOW_START[0] + T)], BF16, name="windows", tag="window0", align_bytes=64)
+        cast(0)
+        picked0 = [keep.tile([P, 4 * 512], BF16, name="picked0_%d" % h, align_bytes=64) for h in range(2)]
+        for h in range(2):
+            nc.vector.tensor_copy(out=word_pairs(picked0[h])[:, :, 0], in_=looked_up(0, 512 * h, 512))
+        cast(1)
+        for h in range(2):
+            nc.vector.tensor_copy(out=word_pairs(picked0[h])[:, :, 1], in_=looked_up(1, 512 * h, 512))
+        for h in range(2):
+            quantize(0, 512 * h, 512, picked0[h][:])
+        cast(2)
+
+        picked1 = [
+            keep.tile([P, 4 * QUARTER], BF16, name="picked1_%d" % q, tag="picked1_%d" % q, align_bytes=64) for q in range(4)
+        ]
+        apart = {q: keep.tile([P, 2, QUARTER], U32, name="apart%d" % q) for q in (1, 2, 3)}
+
+        def gather1(u, q):
+            dst = apart[q][:, u, :] if q in apart else word_pairs(picked1[q])[:, :, u]
+            nc.vector.tensor_copy(out=dst, in_=looked_up(2 + u, QUARTER * q, QUARTER))
+
+        for q in range(4):
+            gather1(0, q)
+        cast(3)
+        w_words = keep.tile([P, PASSES, 2 * N], U8, name="w_words", tag="raw3_0", align_bytes=64)
+        nc.sync.dma_start(out=w_words[:].bitcast(I32), in_=w1_words.rearrange("z p c -> p z c").bitcast(I32))
+        for i in (0, 2, 3, 4, 5, 1, 6):
+            multiply(i, 0)
+        for q in (1, 2, 3, 0):
+            gather1(1, q)
+            if q in apart:
+                nc.scalar.copy(out=word_pairs(picked1[q]), in_=apart[q][:].rearrange("p u s -> p s u"))
+        for q in (1, 0, 2, 3):
+            quantize(1, QUARTER * q, QUARTER, picked1[q][:])
+        for i in (0, 2, 3, 4, 5, 1, 6):
+            multiply(i, 1)
+
+        y = [keep.tile([P, S], F32, name="y%d" % b, tag=("picked1_3", "codes1")[b], align_bytes=64) for b in range(BLOCKS)]
+        for i in (0, 2, 3, 4, 5, 1, 6):
+            b, first, count = groups[i]
+            if count == 512:
+                nc.scalar.copy(out=y[b][:, first : first + count], in_=acc[i][:])
+            else:
+                nc.vector.tensor_copy(out=y[b][:, first : first + count], in_=acc[i][:])
+
+        def neighbours(b, h, d):
+            return y[b][:].indirect(pos_sb[d][:, 16 * h : 16 * (h + 1)])
+
+        def store(b, h, result):
+            nc.sync.dma_start(out=out[P * b : P * (b + 1), HALF_V * h : HALF_V * (h + 1)], in_=result[:])
+
+        turn_banks = (7, 0, 2)
+        sum_banks = ((4, 5), (3, 6), (4, 5))
+        step = 0
+        for piece in range(3):
+            b, h = divmod(piece, 2)
+            sums = [bank(sum_banks[piece][c], [P, P], "sum%d_%d" % (piece, c)) for c in range(2)]
+            for d in range(D):
+                got = keep.tile([P, HALF_V], F32, name="got%d_%d" % (piece, d))
+                nc.vector.tensor_copy(out=got[:], in_=neighbours(b, h, d))
+                turned = bank(turn_banks[step % 3], [P, 2, P], "turned%d" % step)
+                for c in range(2):
+                    nc.tensor.transpose(turned[:, c, :], got[:, P * c : P * (c + 1)], ident[:])
+                scaled = keep.tile([P, 2, P], F32, name="scaled%d_%d" % (piece, d))
+                for c in range(2):
+                    factor = weight[:, d, 2 * h + c : 2 * h + c + 1]
+                    nc.scalar.activation(out=scaled[:, c, :], in_=turned[:, c, :], func=ACT.Copy, scale=factor)
+                for c in range(2):
+                    nc.tensor.matmul(
+                        sums[c][:], scaled[:, c, :], ident[:], start=(d == 0), stop=(d == D - 1), is_transpose=True
+                    )
+                step = step + 1
+            result = keep.tile([P, HALF_V], F32, name="result%d" % piece)
+            for c in range(2):
+                nc.scalar.activation(out=result[:, P * c : P * (c + 1)], in_=sums[c][:], func=ACT.Relu)
+            store(b, h, result)
+
+        terms = [keep.tile([P, HALF_V], F32, name="term%d" % d) for d in range(D)]
+        for d in range(D):
+            nc.vector.tensor_tensor(terms[d][:], neighbours(1, 1, d), spread[d][:], ALU.mult)
+        two = keep.tile([P, HALF_V], F32, name="two")
+        three = keep.tile([P, HALF_V], F32, name="three")
+        result = keep.tile([P, HALF_V], F32, name="result3")
+        halves = [slice(0, P), slice(P, 2 * P)]
+        for cols in halves:
+            nc.vector.tensor_tensor(two[:, cols], terms[0][:, cols], terms[1][:, cols], ALU.add)
+        for cols in halves:
+            nc.vector.tensor_tensor(three[:, cols], two[:, cols], terms[2][:, cols], ALU.add)
+        for cols in halves:
+            nc.vector.tensor_scalar(result[:, cols], three[:, cols], 0.0, None, ALU.max)
+        store(1, 1, result)

@@ -27,10 +27,10 @@ HALF_V = V // 2
 CHUNKS = (
     ((1024, 0), (1024, 320)),
     ((1024, 1024), (1024, 320)),
-    ((1024, 1024), (1024, 320)),
-    ((1024, 896), (512, 0), (256, 0), (256, 96)),
+    ((1024, 1024), (1024, 680)),
+    ((512, 512), (512, 512), (512, 512), (256, 0), (256, 96)),
 )
-WINDOW_START = (3584, 2240, 896, 0)
+WINDOW_START = (4584, 3240, 1536, 0)
 
 
 def tile_picked_gatv_relu_e_kernel(
@@ -105,23 +105,37 @@ def tile_picked_gatv_relu_e_kernel(
         def word_pairs(t):
             return t[:].bitcast(U32).rearrange("p (s u) -> p s u", u=2)
 
-        codes = [keep.tile([P, S], U32, name="codes%d" % z, tag="codes%d" % z, align_bytes=64) for z in range(PASSES)]
+        codes = {}
         x_scales = [keep.tile([P, S], U8, name="x_scales%d" % z, align_bytes=64) for z in range(PASSES)]
 
+        def codes_of(z, first, count):
+            return codes[z, first // 512][:, first % 512 : first % 512 + count].bitcast(FP8X4)
+
         def quantize(z, first, count, src):
-            cols = slice(first, first + count)
-            nc.vector.quantize_mx(out=codes[z][:, cols].bitcast(FP8X4), scales=x_scales[z][:, cols], in_=src)
+            if (z, first // 512) not in codes:
+                tag = "picked1_0" if (z, first // 512) == (1, 1) else "codes%d_%d" % (z, first // 512)
+                codes[z, first // 512] = keep.tile([P, 512], U32, name="codes%d_%d" % (z, first // 512), tag=tag, align_bytes=64)
+            nc.vector.quantize_mx(out=codes_of(z, first, count), scales=x_scales[z][:, first : first + count], in_=src)
 
         groups = [(0, 0, 512), (1, 0, 512), (0, 512, 128), (0, 640, 128), (0, 768, 128), (0, 896, 128), (1, 512, 512)]
+
+        w_words = {}
+
+        def load_words(z, first, count, tag):
+            t = keep.tile([P, 2 * P * count], U8, name="w_words%d_%d" % (z, first), tag=tag, align_bytes=64)
+            words = w1_words[z, :, 2 * P * first : 2 * P * (first + count)]
+            nc.sync.dma_start(out=t[:].bitcast(I32), in_=words.bitcast(I32))
+            for b in range(count):
+                w_words[z, first + b] = t[:, 2 * P * b : 2 * P * (b + 1)]
 
         def multiply(i, z):
             b, first, count = groups[i]
             cols = slice(first, first + count)
             nc.tensor.matmul_mx(
                 out=acc[i][:],
-                lhsT=w_words[:, z, 2 * P * b : 2 * P * (b + 1)].bitcast(FP4X4),
+                lhsT=w_words[z, b].bitcast(FP4X4),
                 lhsT_scale=w_scales[:, z, P * b : P * (b + 1)],
-                rhs=codes[z][:, cols].bitcast(FP8X4),
+                rhs=codes_of(z, first, count),
                 rhs_scale=x_scales[z][:, cols],
                 start=(z == 0),
                 stop=(z == PASSES - 1),
@@ -169,7 +183,7 @@ def tile_picked_gatv_relu_e_kernel(
         picked1 = [
             keep.tile([P, 4 * QUARTER], BF16, name="picked1_%d" % q, tag="picked1_%d" % q, align_bytes=64) for q in range(4)
         ]
-        apart = {q: keep.tile([P, 2, QUARTER], U32, name="apart%d" % q) for q in (1, 2, 3)}
+        apart = {q: keep.tile([P, 2, QUARTER], U32, name="apart%d" % q) for q in (0, 1, 2)}
 
         def gather1(u, q):
             dst = apart[q][:, u, :] if q in apart else word_pairs(picked1[q])[:, :, u]
@@ -178,21 +192,22 @@ def tile_picked_gatv_relu_e_kernel(
         for q in range(4):
             gather1(0, q)
         cast(3)
-        w_words = keep.tile([P, PASSES, 2 * N], U8, name="w_words", tag="raw3_0", align_bytes=64)
-        nc.sync.dma_start(out=w_words[:].bitcast(I32), in_=w1_words.rearrange("z p c -> p z c").bitcast(I32))
+        load_words(1, 0, 1, "w_words1_0")
+        load_words(0, 0, 2, "raw3_1")
         for i in (0, 2, 3, 4, 5, 1, 6):
             multiply(i, 0)
-        for q in (1, 2, 3, 0):
+        for q in range(4):
             gather1(1, q)
             if q in apart:
                 nc.scalar.copy(out=word_pairs(picked1[q]), in_=apart[q][:].rearrange("p u s -> p s u"))
-        for q in (1, 0, 2, 3):
+        for q in (0, 1, 3, 2):
             quantize(1, QUARTER * q, QUARTER, picked1[q][:])
-        for i in (0, 2, 3, 4, 5, 1, 6):
+        load_words(1, 1, 1, "picked1_3")
+        for i in (4, 5, 0, 2, 3, 1, 6):
             multiply(i, 1)
 
-        y = [keep.tile([P, S], F32, name="y%d" % b, tag=("picked1_3", "codes1")[b], align_bytes=64) for b in range(BLOCKS)]
-        for i in (0, 2, 3, 4, 5, 1, 6):
+        y = [keep.tile([P, S], F32, name="y%d" % b, tag=("picked1_2", "picked1_0")[b], align_bytes=64) for b in range(BLOCKS)]
+        for i in (0, 4, 5, 2, 3, 1, 6):
             b, first, count = groups[i]
             if count == 512:
                 nc.scalar.copy(out=y[b][:, first : first + count], in_=acc[i][:])

@@ -25,12 +25,12 @@ QUARTER = S // 4
 HALF_V = V // 2
 
 CHUNKS = (
-    ((1024, 0), (1024, 320)),
-    ((1024, 1024), (1024, 320)),
-    ((1024, 1024), (1024, 680)),
+    ((1024, 512), (1024, 320)),
+    ((768, 768), (768, 768), (512, 0)),
+    ((768, 768), (768, 768), (512, 192)),
     ((512, 512), (512, 512), (512, 512), (256, 0), (256, 96)),
 )
-WINDOW_START = (4584, 3240, 1536, 0)
+WINDOW_START = (4608, 3072, 1536, 0)
 
 
 def tile_picked_gatv_relu_e_kernel(
@@ -74,29 +74,23 @@ def tile_picked_gatv_relu_e_kernel(
         load_x(0, 0)
         load_x(0, 1)
         nc.sync.dma_start(offs_sb[:], offs)
-        load_x(1, 0)
-        load_scales(0)
-        load_scales(1)
-        load_x(1, 1)
-        load_scales(2)
-        load_scales(3)
-        load_x(2, 0)
-        load_x(2, 1)
-        for i in range(len(CHUNKS[3])):
-            load_x(3, i)
-        for d, pos in enumerate((pos1, pos2, pos3)):
-            nc.sync.dma_start(pos_sb[d][:], pos)
+        for pair in range(1, 4):
+            for i in range(len(CHUNKS[pair])):
+                load_x(pair, i)
+        for q in range(4):
+            load_scales(q)
 
         def cast(pair):
             for i, (width, on_scalar) in enumerate(CHUNKS[pair]):
                 t, start = raw[pair, i]
-                src = t[:].rearrange("p e c -> p c e")
+                src = t[:].rearrange("p e (c i) -> p c e i", i=4)
                 first = WINDOW_START[pair] + start
-                dst = windows[:, 2 * first : 2 * (first + width)].rearrange("p (c e) -> p c e", e=2)
+                dst = windows[:, 2 * first : 2 * (first + width)].rearrange("p (c i e) -> p c e i", i=4, e=2)
+                cut = on_scalar // 4
                 if on_scalar > 0:
-                    nc.scalar.copy(out=dst[:, :on_scalar, :], in_=src[:, :on_scalar, :])
+                    nc.scalar.copy(out=dst[:, :cut], in_=src[:, :cut])
                 if on_scalar < width:
-                    nc.vector.tensor_copy(out=dst[:, on_scalar:, :], in_=src[:, on_scalar:, :])
+                    nc.vector.tensor_copy(out=dst[:, cut:], in_=src[:, cut:])
 
         def looked_up(pair, first, count):
             words = windows[:, 2 * WINDOW_START[pair] : 2 * (WINDOW_START[pair] + T)].bitcast(U32)
@@ -194,12 +188,17 @@ def tile_picked_gatv_relu_e_kernel(
         cast(3)
         load_words(1, 0, 1, "w_words1_0")
         load_words(0, 0, 2, "raw3_1")
+        for d, pos in enumerate((pos1, pos2, pos3)):
+            nc.sync.dma_start(pos_sb[d][:], pos)
         for i in (0, 2, 3, 4, 5, 1, 6):
             multiply(i, 0)
         for q in range(4):
             gather1(1, q)
             if q in apart:
-                nc.scalar.copy(out=word_pairs(picked1[q]), in_=apart[q][:].rearrange("p u s -> p s u"))
+                nc.scalar.copy(
+                    out=picked1[q][:].bitcast(U32).rearrange("p (s i u) -> p s u i", i=4, u=2),
+                    in_=apart[q][:].rearrange("p u (s i) -> p s u i", i=4),
+                )
         for q in (0, 1, 3, 2):
             quantize(1, QUARTER * q, QUARTER, picked1[q][:])
         load_words(1, 1, 1, "picked1_3")
@@ -207,12 +206,16 @@ def tile_picked_gatv_relu_e_kernel(
             multiply(i, 1)
 
         y = [keep.tile([P, S], F32, name="y%d" % b, tag=("picked1_2", "picked1_0")[b], align_bytes=64) for b in range(BLOCKS)]
-        for i in (0, 4, 5, 2, 3, 1, 6):
+
+        def empty(i):
             b, first, count = groups[i]
             if count == 512:
                 nc.scalar.copy(out=y[b][:, first : first + count], in_=acc[i][:])
             else:
                 nc.vector.tensor_copy(out=y[b][:, first : first + count], in_=acc[i][:])
+
+        for i in (0, 4, 5, 2, 3):
+            empty(i)
 
         def neighbours(b, h, d):
             return y[b][:].indirect(pos_sb[d][:, 16 * h : 16 * (h + 1)])
@@ -220,8 +223,8 @@ def tile_picked_gatv_relu_e_kernel(
         def store(b, h, result):
             nc.sync.dma_start(out=out[P * b : P * (b + 1), HALF_V * h : HALF_V * (h + 1)], in_=result[:])
 
-        turn_banks = (7, 0, 2)
-        sum_banks = ((4, 5), (3, 6), (4, 5))
+        turn_banks = (7, 0, 2, 3)
+        sum_banks = ((4, 5), (1, 6), (4, 5))
         step = 0
         for piece in range(3):
             b, h = divmod(piece, 2)
@@ -229,7 +232,7 @@ def tile_picked_gatv_relu_e_kernel(
             for d in range(D):
                 got = keep.tile([P, HALF_V], F32, name="got%d_%d" % (piece, d))
                 nc.vector.tensor_copy(out=got[:], in_=neighbours(b, h, d))
-                turned = bank(turn_banks[step % 3], [P, 2, P], "turned%d" % step)
+                turned = bank(turn_banks[step % 4], [P, 2, P], "turned%d" % step)
                 for c in range(2):
                     nc.tensor.transpose(turned[:, c, :], got[:, P * c : P * (c + 1)], ident[:])
                 scaled = keep.tile([P, 2, P], F32, name="scaled%d_%d" % (piece, d))
@@ -240,6 +243,8 @@ def tile_picked_gatv_relu_e_kernel(
                     nc.tensor.matmul(
                         sums[c][:], scaled[:, c, :], ident[:], start=(d == 0), stop=(d == D - 1), is_transpose=True
                     )
+                if step < 2:
+                    empty((1, 6)[step])
                 step = step + 1
             result = keep.tile([P, HALF_V], F32, name="result%d" % piece)
             for c in range(2):

from contextlib import ExitStack

import concourse.mybir as mybir
from concourse.masks import make_identity

K, T, S, D, V, N = 1024, 2048, 1024, 3, 512, 256
FLOPS = 2 * K * S * N

F32 = mybir.dt.float32
BF16 = mybir.dt.bfloat16
I32 = mybir.dt.int32
U32 = mybir.dt.uint32
U16 = mybir.dt.uint16
U8 = mybir.dt.uint8
FP8X4 = mybir.dt.float8_e4m3fn_x4
FP4X4 = mybir.dt.float4_e2m1fn_x4
ALU = mybir.AluOpType
ACT = mybir.ActivationFunctionType
AX = mybir.AxisListType

P = 128
PASSES = 2
BLOCKS = N // P
QUARTER = S // 4
HALF_V = V // 2

CHUNKS = (
    ((1024, 512), (1024, 320)),
    ((768, 768), (768, 768), (512, 0)),
    ((768, 768), (768, 768), (512, 192)),
    ((512, 512), (512, 512), (512, 512), (256, 0), (256, 96)),
)
WINDOW_START = (4608, 3072, 1536, 0)


def tile_picked_gatv_relu_e_kernel(
    tc, xT, w1_words, w1_scales, score, offs, pos1, pos2, pos3, out
):
    nc = tc.nc
    with ExitStack() as ctx:
        keep = ctx.enter_context(tc.tile_pool(name="keep", bufs=1))
        psum = ctx.enter_context(tc.psum_pool(name="psum", bufs=1))

        def bank(i, shape, name):
            return psum.tile(shape, F32, tag="bank%d" % i, name=name)

        offs_sb = keep.tile([P, S // 16], U16, name="offs_sb")
        pos_sb = [keep.tile([P, V // 16], U16, name="pos_sb%d" % d) for d in range(D)]
        w_scales = keep.tile([P, PASSES, N], U8, name="w_scales", align_bytes=64)
        score_rows = keep.tile([P, P], F32, name="score_rows")
        ident = keep.tile([P, P], F32, name="ident")

        nc.gpsimd.memset(w_scales[:].bitcast(I32), 0)
        make_identity(nc, ident[:])

        x_rows = xT.rearrange("(z p u e) t -> z u p e t", z=PASSES, p=P, u=2, e=2)
        raw = {}

        def load_x(pair, i):
            start = sum(c[0] for c in CHUNKS[pair][:i])
            width = CHUNKS[pair][i][0]
            t = keep.tile([P, 2, width], F32, name="raw%d_%d" % (pair, i), tag="raw%d_%d" % (pair, i), align_bytes=64)
            nc.sync.dma_start(out=t[:], in_=x_rows[pair // 2, pair % 2, :, :, start : start + width])
            raw[pair, i] = (t, start)

        def load_scales(q):
            nc.sync.dma_start(
                out=w_scales[32 * q : 32 * q + 4, :, :].bitcast(I32),
                in_=w1_scales[:, 4 * q : 4 * q + 4, :].rearrange("z r c -> r z c").bitcast(I32),
            )

        score_runs = score.rearrange("d r (c p) -> (d r c) p", p=P)
        nc.sync.dma_start(out=score_rows[:], in_=score_runs[0 : 9 * (P - 1) + 1 : 9, :])
        load_x(0, 0)
        load_x(0, 1)
        nc.sync.dma_start(offs_sb[:], offs)
        for pair in range(1, 4):
            for i in range(len(CHUNKS[pair])):
                load_x(pair, i)
        for q in range(4):
            load_scales(q)

        def cast(pair):
            for i, (width, on_scalar) in enumerate(CHUNKS[pair]):
                t, start = raw[pair, i]
                src = t[:].rearrange("p e (c i) -> p c e i", i=4)
                first = WINDOW_START[pair] + start
                dst = windows[:, 2 * first : 2 * (first + width)].rearrange("p (c i e) -> p c e i", i=4, e=2)
                cut = on_scalar // 4
                if on_scalar > 0:
                    nc.scalar.copy(out=dst[:, :cut], in_=src[:, :cut])
                if on_scalar < width:
                    nc.vector.tensor_copy(out=dst[:, cut:], in_=src[:, cut:])

        def looked_up(pair, first, count):
            words = windows[:, 2 * WINDOW_START[pair] : 2 * (WINDOW_START[pair] + T)].bitcast(U32)
            return words.indirect(offs_sb[:, first // 16 : (first + count) // 16])

        def word_pairs(t):
            return t[:].bitcast(U32).rearrange("p (s u) -> p s u", u=2)

        codes = {}
        x_scales = [keep.tile([P, S], U8, name="x_scales%d" % z, align_bytes=64) for z in range(PASSES)]

        def codes_of(z, first, count):
            return codes[z, first // 512][:, first % 512 : first % 512 + count].bitcast(FP8X4)

        def quantize(z, first, count, src):
            if (z, first // 512) not in codes:
                tag = "picked1_0" if (z, first // 512) == (1, 1) else "codes%d_%d" % (z, first // 512)
                codes[z, first // 512] = keep.tile([P, 512], U32, name="codes%d_%d" % (z, first // 512), tag=tag, align_bytes=64)
            nc.vector.quantize_mx(out=codes_of(z, first, count), scales=x_scales[z][:, first : first + count], in_=src)

        groups = [(0, 0, 512), (1, 0, 512), (0, 512, 128), (0, 640, 128), (0, 768, 128), (0, 896, 128), (1, 512, 512)]

        w_words = {}

        def load_words(z, first, count, tag):
            t = keep.tile([P, 2 * P * count], U8, name="w_words%d_%d" % (z, first), tag=tag, align_bytes=64)
            words = w1_words[z, :, 2 * P * first : 2 * P * (first + count)]
            nc.sync.dma_start(out=t[:].bitcast(I32), in_=words.bitcast(I32))
            for b in range(count):
                w_words[z, first + b] = t[:, 2 * P * b : 2 * P * (b + 1)]

        def multiply(i, z):
            b, first, count = groups[i]
            cols = slice(first, first + count)
            nc.tensor.matmul_mx(
                out=acc[i][:],
                lhsT=w_words[z, b].bitcast(FP4X4),
                lhsT_scale=w_scales[:, z, P * b : P * (b + 1)],
                rhs=codes_of(z, first, count),
                rhs_scale=x_scales[z][:, cols],
                start=(z == 0),
                stop=(z == PASSES - 1),
            )

        score_t = bank(7, [P, D, 60], "score_t")
        nc.tensor.transpose(score_t[:].rearrange("p d j -> p (d j)")[:, 0:P], score_rows[:], ident[:])
        top = keep.tile([P, 4], F32, name="top")
        shifted = keep.tile([P, D, 4], F32, name="shifted")
        expo = keep.tile([P, D, 4], F32, name="expo")
        total = keep.tile([P, 4], F32, name="total")
        inverse = keep.tile([P, 4], F32, name="inverse", tag="window0", align_bytes=64)
        weight = keep.tile([P, D, 4], F32, name="weight")
        nc.vector.tensor_reduce(out=top[:], in_=score_t[:, :, 0:4].rearrange("p d c -> p c d"), axis=AX.X, op=ALU.max)
        nc.vector.tensor_tensor(
            out=shifted[:], in0=score_t[:, :, 0:4], in1=top[:].unsqueeze(1).to_broadcast([P, D, 4]), op=ALU.subtract
        )
        nc.scalar.activation(out=expo[:], in_=shifted[:], func=ACT.Exp)
        nc.vector.tensor_reduce(out=total[:], in_=expo[:].rearrange("p d c -> p c d"), axis=AX.X, op=ALU.add)
        nc.vector.reciprocal(out=inverse[:], in_=total[:])
        nc.vector.tensor_tensor(
            out=weight[:], in0=expo[:], in1=inverse[:].unsqueeze(1).to_broadcast([P, D, 4]), op=ALU.mult
        )

        spread = [keep.tile([P, HALF_V], F32, name="spread%d" % d) for d in range(D)]
        for d in range(D):
            spread_t = bank(d, [P, HALF_V], "spread_t%d" % d)
            for c in range(2):
                nc.tensor.transpose(spread_t[:, P * c : P * (c + 1)], weight[:, d, 2 + c : 3 + c].to_broadcast([P, P]), ident[:])
            nc.vector.tensor_copy(out=spread[d][:], in_=spread_t[:])

        acc = [bank(i, [P, g[2]], "acc%d" % i) for i, g in enumerate(groups)]
        windows = keep.tile([P, 2 * (WINDOW_START[0] + T)], BF16, name="windows", tag="window0", align_bytes=64)
        cast(0)
        picked0 = [keep.tile([P, 4 * 512], BF16, name="picked0_%d" % h, align_bytes=64) for h in range(2)]
        for h in range(2):
            nc.vector.tensor_copy(out=word_pairs(picked0[h])[:, :, 0], in_=looked_up(0, 512 * h, 512))
        cast(1)
        for h in range(2):
            nc.vector.tensor_copy(out=word_pairs(picked0[h])[:, :, 1], in_=looked_up(1, 512 * h, 512))
        for h in range(2):
            quantize(0, 512 * h, 512, picked0[h][:])
        cast(2)

        picked1 = [
            keep.tile([P, 4 * QUARTER], BF16, name="picked1_%d" % q, tag="picked1_%d" % q, align_bytes=64) for q in range(4)
        ]
        apart = {q: keep.tile([P, 2, QUARTER], U32, name="apart%d" % q) for q in (0, 1, 2)}

        def gather1(u, q):
            dst = apart[q][:, u, :] if q in apart else word_pairs(picked1[q])[:, :, u]
            nc.vector.tensor_copy(out=dst, in_=looked_up(2 + u, QUARTER * q, QUARTER))

        for q in range(4):
            gather1(0, q)
        cast(3)
        load_words(1, 0, 1, "w_words1_0")
        load_words(0, 0, 2, "raw3_1")
        for d, pos in enumerate((pos1, pos2, pos3)):
            nc.sync.dma_start(pos_sb[d][:], pos)
        for i in (0, 2, 3, 4, 5, 1, 6):
            multiply(i, 0)
        for q in range(4):
            gather1(1, q)
            if q in apart:
                nc.scalar.copy(
                    out=picked1[q][:].bitcast(U32).rearrange("p (s i u) -> p s u i", i=4, u=2),
                    in_=apart[q][:].rearrange("p u (s i) -> p s u i", i=4),
                )
        for q in (0, 1, 3, 2):
            quantize(1, QUARTER * q, QUARTER, picked1[q][:])
        load_words(1, 1, 1, "picked1_3")
        for i in (4, 5, 0, 2, 3, 1, 6):
            multiply(i, 1)

        y = [keep.tile([P, S], F32, name="y%d" % b, tag=("picked1_2", "picked1_0")[b], align_bytes=64) for b in range(BLOCKS)]

        def empty(i):
            b, first, count = groups[i]
            if count == 512:
                nc.scalar.copy(out=y[b][:, first : first + count], in_=acc[i][:])
            else:
                nc.vector.tensor_copy(out=y[b][:, first : first + count], in_=acc[i][:])

        for i in (0, 4, 5, 2, 3):
            empty(i)

        def neighbours(b, h, d):
            return y[b][:].indirect(pos_sb[d][:, 16 * h : 16 * (h + 1)])

        def store(b, h, result):
            nc.sync.dma_start(out=out[P * b : P * (b + 1), HALF_V * h : HALF_V * (h + 1)], in_=result[:])

        turn_banks = (7, 0, 2, 3)
        sum_banks = ((4, 5), (1, 6), (4, 5))
        step = 0
        for piece in range(3):
            b, h = divmod(piece, 2)
            sums = [bank(sum_banks[piece][c], [P, P], "sum%d_%d" % (piece, c)) for c in range(2)]
            for d in range(D):
                got = keep.tile([P, HALF_V], F32, name="got%d_%d" % (piece, d))
                nc.vector.tensor_copy(out=got[:], in_=neighbours(b, h, d))
                turned = bank(turn_banks[step % 4], [P, 2, P], "turned%d" % step)
                for c in range(2):
                    nc.tensor.transpose(turned[:, c, :], got[:, P * c : P * (c + 1)], ident[:])
                scaled = keep.tile([P, 2, P], F32, name="scaled%d_%d" % (piece, d))
                for c in range(2):
                    factor = weight[:, d, 2 * h + c : 2 * h + c + 1]
                    nc.scalar.activation(out=scaled[:, c, :], in_=turned[:, c, :], func=ACT.Copy, scale=factor)
                for c in range(2):
                    nc.tensor.matmul(
                        sums[c][:], scaled[:, c, :], ident[:], start=(d == 0), stop=(d == D - 1), is_transpose=True
                    )
                if step < 2:
                    empty((1, 6)[step])
                step = step + 1
            result = keep.tile([P, HALF_V], F32, name="result%d" % piece)
            for c in range(2):
                nc.scalar.activation(out=result[:, P * c : P * (c + 1)], in_=sums[c][:], func=ACT.Relu)
            store(b, h, result)

        terms = [keep.tile([P, HALF_V], F32, name="term%d" % d) for d in range(D)]
        for d in range(D):
            nc.vector.tensor_tensor(terms[d][:], neighbours(1, 1, d), spread[d][:], ALU.mult)
        two = keep.tile([P, HALF_V], F32, name="two")
        three = keep.tile([P, HALF_V], F32, name="three")
        result = keep.tile([P, HALF_V], F32, name="result3")
        halves = [slice(0, P), slice(P, 2 * P)]
        for cols in halves:
            nc.vector.tensor_tensor(two[:, cols], terms[0][:, cols], terms[1][:, cols], ALU.add)
        for cols in halves:
            nc.vector.tensor_tensor(three[:, cols], two[:, cols], terms[2][:, cols], ALU.add)
        for cols in halves:
            nc.vector.tensor_scalar(result[:, cols], three[:, cols], 0.0, None, ALU.max)
        store(1, 1, result)
